import numpy as np
import ml_dtypes


def mxq(x, axis, fmt="e4m3"):
    dtype, down = {"e4m3": (ml_dtypes.float8_e4m3fn, 7), "e5m2": (ml_dtypes.float8_e5m2, 14)}[fmt]
    v = np.moveaxis(np.asarray(x, np.float32).astype(ml_dtypes.bfloat16).astype(np.float64), axis, -1)
    blocks = v.reshape(v.shape[:-1] + (-1, 32))
    amax = np.abs(blocks).max(-1, keepdims=True)
    byte = np.maximum(np.where(amax > 0, np.frexp(amax)[1] - 1 + 127, 0) - down, 1)
    scale = np.exp2(byte - 127.0)
    codes = (blocks / scale).astype(np.float32).astype(dtype).astype(np.float64)
    return np.moveaxis((codes * scale).reshape(v.shape), -1, axis)


WIDE = False


def mx_kscale(k):
    if not WIDE:
        return np.ones(k)
    levels = np.array([10, -10, 5, -5, 0])
    if k % 512:
        return np.exp2(np.random.permutation(np.resize(levels, k // 32))).repeat(32)
    a = np.empty((k // 512, 16))
    for p in range(k // 512):
        a[p, :8] = np.random.permutation(np.resize(levels, 8))
        for g in range(8):
            far = levels[np.abs(levels - a[p, g]) >= 10]
            a[p, g + 8] = far[np.random.randint(len(far))]
    return np.exp2(a.ravel()).repeat(32)


def f64(x):
    return np.asarray(x).astype(np.float64)


def striped(idx):
    return np.tile(idx.reshape(-1, 16).T, (8, 1)).astype(np.uint16)


def unstriped(offs):
    return offs[:16].T.reshape(-1).astype(np.int64)


def pack_weight(w):
    k, n = w.shape
    w = f64(np.asarray(w, np.float32).astype(ml_dtypes.bfloat16)).reshape(k // 32, 32, n)
    amax = np.abs(w).max(1)
    byte = np.clip(np.where(amax > 0, np.frexp(amax)[1] - 1 + 127 - 7, 1), 1, 254)
    scaled = (w * np.exp2(127.0 - byte)[:, None, :]).reshape(k, n).astype(np.float32)
    words = np.ascontiguousarray(scaled.reshape(k // 512, 128, 4, n).transpose(0, 1, 3, 2)).astype(ml_dtypes.float8_e4m3fn).view(np.uint8)
    return words, np.ascontiguousarray(byte.astype(np.uint8).reshape(k // 512, 16, n))


def unpack_weight(words, scales):
    g, p, n, _ = words.shape
    vals = np.ascontiguousarray(words).view(ml_dtypes.float8_e4m3fn).astype(np.float64) * np.repeat(np.exp2(scales.astype(np.float64) - 127.0), 8, axis=1)[..., None]
    return vals.transpose(0, 1, 3, 2).reshape(g * 512, n)


def relu(v):
    return np.maximum(v, 0.0)


K, T, S, N, H = 512, 2048, 512, 256, 512


def setup_inputs():
    n = np.random.standard_normal
    s = mx_kscale(K)[:, None]
    u = mx_kscale(H)
    packed_xT = pack_weight(n((K, T)) * s)
    return {
        "x_words": packed_xT[0],
        "x_scales": packed_xT[1],
        "w1": (n((K, H)) / np.sqrt(K) / s).astype(np.float32),
        "w2": (n((K, H)) / np.sqrt(K) / s).astype(np.float32),
        "wind": (np.random.uniform(0.2, 1.2, (H, S))).astype(np.float32),
        "unit": (np.random.uniform(0.6, 1.4, (H, 1)) * u[:, None]).astype(np.float32),
        "w3": (n((H, N)) / np.sqrt(H) / u[:, None]).astype(np.float32),
        "offs": striped(np.random.permutation(T)[:S]),
        "stn": striped(np.random.permutation(S)),
    }


def reference(x_words, x_scales, w1, w2, wind, unit, w3, offs, stn):
    xq = unpack_weight(x_words, x_scales)[:, unstriped(offs)]
    tm = mxq(f64(w1), 0, "e4m3").T @ xq
    es = np.exp(0.8 * np.tanh(tm))
    dlt = es / ((0.3 * np.tanh(tm) + 1.3) ** 2)
    rd = mxq(f64(w2), 0, "e4m3").T @ xq
    rn = np.log(np.exp(rd) + 1.0)
    gam = 0.3 * f64(wind) + 0.5
    ed = es[:, unstriped(stn)]
    vpd = relu(es - (0.6 * ed))
    et = (dlt * rn + (gam * f64(wind)) * vpd) / (dlt + gam)
    hid = f64(unit) * et
    return mxq(f64(w3), 0, "e4m3").T @ mxq(hid, 0, "e4m3")

@@ -1,0 +1,220 @@
+from contextlib import ExitStack
+
+import concourse.mybir as mybir
+
+K, T, S, N, H = 512, 2048, 512, 256, 512
+FLOPS = 2 * K * H * S * 2 + 2 * H * N * S
+
+F32 = mybir.dt.float32
+BF16 = mybir.dt.bfloat16
+I32 = mybir.dt.int32
+U32 = mybir.dt.uint32
+U16 = mybir.dt.uint16
+U8 = mybir.dt.uint8
+FP8X4 = mybir.dt.float8_e4m3fn_x4
+ACT = mybir.ActivationFunctionType
+ALU = mybir.AluOpType
+
+P = 128
+PACK = 4
+LIST_ROWS = 16
+CHUNK = 128
+SCALAR_CAST = 64
+
+
+def tile_picked_ypenman_et_p_kernel(
+    tc, x_words, x_scales, w1, w2, wind, unit, w3, offs, stn, out
+):
+    nc = tc.nc
+    with ExitStack() as ctx:
+        keep = ctx.enter_context(tc.tile_pool(name="keep", bufs=1))
+        psum = ctx.enter_context(tc.psum_pool(name="psum", bufs=1))
+
+        def rows(name):
+            return keep.tile([P, PACK, S], F32, name=name)
+
+        offs_sb = keep.tile([P, S // LIST_ROWS], U16, name="offs_sb")
+        nc.sync.dma_start(offs_sb[:], offs)
+        stn_sb = keep.tile([P, S // LIST_ROWS], U16, name="stn_sb")
+        nc.sync.dma_start(stn_sb[:], stn)
+
+        w1_raw = keep.tile([P, PACK, H], F32, name="w1_raw", tag="raw")
+        nc.sync.dma_start(w1_raw[:], w1.rearrange("(p j) c -> p j c", j=PACK))
+
+        scale_table = keep.tile([P, T], U8, name="scale_table")
+        nc.gpsimd.memset(scale_table[:].bitcast(I32), 0)
+        for q in range(4):
+            nc.sync.dma_start(
+                scale_table[32 * q : 32 * q + 4, :].bitcast(I32),
+                x_scales[0, 4 * q : 4 * q + 4, :].bitcast(I32),
+            )
+        word_table = keep.tile([P, T], I32, name="word_table", tag="words_then_weights")
+        nc.sync.dma_start(word_table[:], x_words[0].rearrange("p n t -> p (n t)").bitcast(I32))
+        unit_sb = keep.tile([P, PACK], F32, name="unit_sb")
+        nc.sync.dma_start(unit_sb[:], unit.rearrange("(p t) o -> p (t o)", t=PACK))
+
+        def quantise(grouped, width, name):
+            codes = keep.tile([P, width], U32, name=name + "_codes", align_bytes=64)
+            scales = keep.tile([P, width], U8, name=name + "_scales", align_bytes=64)
+            nc.vector.quantize_mx(out=codes[:].bitcast(FP8X4), scales=scales[:], in_=grouped)
+            return codes, scales
+
+        def dealt_views(raw, name, tag):
+            grouped = keep.tile([P, PACK * H], BF16, name=name + "_grouped", tag=tag, align_bytes=64)
+            dst = grouped[:].rearrange("p (t m j) -> p m j t", t=PACK, j=PACK)
+            src = raw[:].rearrange("p j (m t) -> p m j t", t=PACK)
+            return grouped, dst, src
+
+        w1_grouped, dst, src = dealt_views(w1_raw, "w1", "grouped_then_wind")
+        nc.scalar.activation(out=dst[:, :SCALAR_CAST], in_=src[:, :SCALAR_CAST], func=ACT.Copy)
+        nc.vector.tensor_copy(out=dst[:, SCALAR_CAST:], in_=src[:, SCALAR_CAST:])
+        w1_codes, w1_scales = quantise(w1_grouped[:], H, "w1")
+
+        w2_raw = keep.tile([P, PACK, H], F32, name="w2_raw", tag="raw")
+        nc.sync.dma_start(w2_raw[:], w2.rearrange("(p j) c -> p j c", j=PACK))
+        wind_sb = keep.tile([P, PACK, S], F32, name="wind_sb", tag="grouped_then_wind", align_bytes=64)
+        nc.sync.dma_start(wind_sb[:], wind.rearrange("(p t) s -> p t s", t=PACK))
+        x_scale = keep.tile([P, S], U8, name="x_scale", align_bytes=64)
+        nc.vector.tensor_copy(out=x_scale[:], in_=scale_table[:].indirect(offs_sb[:]))
+        x_code = keep.tile([P, S], U32, name="x_code", align_bytes=64)
+        nc.vector.tensor_copy(out=x_code[:], in_=word_table[:].bitcast(U32).indirect(offs_sb[:]))
+
+        w3_raw = keep.tile([P, PACK, N], F32, name="w3_raw", tag="words_then_weights")
+        nc.sync.dma_start(w3_raw[:], w3.rearrange("(p j) c -> p j c", j=PACK))
+
+        def first_product(codes, scales, t, tag):
+            acc = psum.tile([P, S], F32, name=tag, tag=tag)
+            cols = slice(t * P, (t + 1) * P)
+            nc.tensor.matmul_mx(
+                out=acc[:], lhsT=codes[:, cols].bitcast(FP8X4), lhsT_scale=scales[:, cols],
+                rhs=x_code[:].bitcast(FP8X4), rhs_scale=x_scale[:], start=True, stop=True,
+            )
+            return acc
+
+        tm = [first_product(w1_codes, w1_scales, t, "tm%d" % t) for t in range(PACK)]
+
+        th, root, ed = rows("th"), rows("root"), rows("ed")
+        h, wh, r, deficit = rows("h"), rows("wh"), rows("r"), rows("deficit")
+        aero, part, den_unit = rows("aero"), rows("part"), rows("den_unit")
+        es = [keep.tile([P, S], F32, name="es%d" % t) for t in range(PACK)]
+
+        w2_grouped, dst, src = dealt_views(w2_raw, "w2", "w2_grouped")
+        nc.vector.tensor_copy(out=dst, in_=src)
+        w2_codes, w2_scales = quantise(w2_grouped[:], H, "w2")
+        rd = [first_product(w2_codes, w2_scales, t, "rd%d" % t) for t in range(PACK)]
+
+        half = S // 2
+        lo, hi = slice(0, 2), slice(2, 4)
+
+        def saturation(t):
+            nc.scalar.activation(out=es[t][:], in_=th[:, t, :], func=ACT.Exp, scale=0.8)
+
+        def other_day(t):
+            for u in range(2):
+                nc.scalar.activation(
+                    out=ed[:, t, u * half : (u + 1) * half],
+                    in_=es[t][:].indirect(stn_sb[:, u * half // LIST_ROWS : (u + 1) * half // LIST_ROWS]),
+                    func=ACT.Copy)
+
+        for t in (0, 1):
+            nc.scalar.activation(out=th[:, t, :], in_=tm[t][:], func=ACT.Tanh)
+        nc.scalar.activation(out=root[:, lo, :], in_=th[:, lo, :], func=ACT.Exp, scale=-0.4)
+        for t in (0, 1):
+            saturation(t)
+        for t in (2, 3):
+            nc.scalar.activation(out=th[:, t, :], in_=tm[t][:], func=ACT.Tanh)
+        for t in (0, 1):
+            other_day(t)
+        nc.scalar.activation(out=h[:, hi, :], in_=th[:, hi, :], func=ACT.Square, scale=0.3 / 1.3, bias=1.0)
+        nc.scalar.activation(out=root[:, hi, :], in_=th[:, hi, :], func=ACT.Exp, scale=-0.8)
+        for t in (2, 3):
+            saturation(t)
+        for t in (2, 3):
+            other_day(t)
+
+        def ratio(pair, last, factor):
+            nc.vector.scalar_tensor_tensor(
+                out=wh[:, pair, :], in0=wind_sb[:, pair, :], scalar=0.5 / 0.3, in1=h[:, pair, :], op0=ALU.add, op1=ALU.mult)
+            for t in range(pair.start, pair.stop):
+                nc.vector.scalar_tensor_tensor(
+                    out=deficit[:, t, :], in0=ed[:, t, :], scalar=-0.6, in1=es[t][:], op0=ALU.mult, op1=ALU.add)
+            nc.vector.scalar_tensor_tensor(
+                out=r[:, pair, :], in0=wh[:, pair, :], scalar=factor, in1=last[:, pair, :], op0=ALU.mult, op1=ALU.mult)
+            nc.vector.scalar_tensor_tensor(
+                out=aero[:, pair, :], in0=deficit[:, pair, :], scalar=0.0, in1=wind_sb[:, pair, :], op0=ALU.max, op1=ALU.mult)
+            for t in range(pair.start, pair.stop):
+                nc.vector.tensor_scalar(
+                    out=den_unit[:, t, :], in0=r[:, t, :], scalar1=-1.0, scalar2=unit_twice[:, t : t + 1],
+                    op0=ALU.is_ge, op1=ALU.mult)
+            nc.vector.tensor_tensor(out=wh[:, pair, :], in0=aero[:, pair, :], in1=r[:, pair, :], op=ALU.mult)
+
+        def partial(pair):
+            for t in range(pair.start, pair.stop):
+                nc.vector.scalar_tensor_tensor(
+                    out=part[:, t, :], in0=rd[t][:], scalar=0.0, in1=wh[:, t, :], op0=ALU.max, op1=ALU.add)
+
+        unit_twice = keep.tile([P, PACK], F32, name="unit_twice")
+        nc.vector.tensor_scalar(out=unit_twice[:], in0=unit_sb[:], scalar1=2.0, scalar2=None, op0=ALU.mult)
+        nc.vector.scalar_tensor_tensor(
+            out=h[:, lo, :], in0=th[:, lo, :], scalar=1.3 / 0.3, in1=root[:, lo, :], op0=ALU.add, op1=ALU.mult)
+        w3_grouped = keep.tile([P, PACK * N], BF16, name="w3_grouped", align_bytes=64)
+        nc.vector.tensor_copy(
+            out=w3_grouped[:].rearrange("p (c i j) -> p c j i", i=4, j=PACK),
+            in_=w3_raw[:].rearrange("p j (c i) -> p c j i", i=4))
+        ratio(lo, h, 0.3 ** 3)
+        w3_codes, w3_scales = quantise(w3_grouped[:], N, "w3")
+        partial(lo)
+        ratio(hi, root, 0.3 * 1.3 ** 2)
+        partial(hi)
+
+        rd_abs, decay = rows("rd_abs"), rows("decay")
+        for t in range(PACK):
+            nc.scalar.activation(out=rd_abs[:, t, :], in_=rd[t][:], func=ACT.Abs)
+        nc.scalar.activation(out=decay[:], in_=rd_abs[:], func=ACT.Exp, scale=-1.0)
+
+        soft = rows("soft")
+        for pair in (lo, hi):
+            nc.scalar.activation(out=soft[:, pair, :], in_=decay[:, pair, :], func=ACT.Ln, bias=1.0)
+
+        num = aero
+        for pair in (lo, hi):
+            nc.vector.tensor_tensor(out=num[:, pair, :], in0=soft[:, pair, :], in1=part[:, pair, :], op=ALU.add)
+        scaled = deficit
+        for t in range(PACK):
+            nc.vector.scalar_tensor_tensor(
+                out=scaled[:, t, :], in0=den_unit[:, t, :], scalar=unit_sb[:, t : t + 1], in1=num[:, t, :],
+                op0=ALU.subtract, op1=ALU.mult)
+
+        inv_sq = rows("inv_sq")
+        chunks = [slice(c * CHUNK, (c + 1) * CHUNK) for c in range(S // CHUNK)]
+        for cols in chunks:
+            nc.scalar.activation(out=decay[:, :, cols], in_=r[:, :, cols], func=ACT.Abs_reciprocal_sqrt, bias=1.0)
+        for cols in chunks:
+            nc.scalar.activation(out=inv_sq[:, :, cols], in_=decay[:, :, cols], func=ACT.Square)
+        hid = [keep.tile([P, PACK * CHUNK], BF16, name="hid%d" % c, align_bytes=64) for c in range(len(chunks))]
+        out_view = out.rearrange("(g m) j -> m g j", m=P)
+
+        def round_hidden(c):
+            nc.vector.tensor_tensor(
+                out=hid[c][:].rearrange("p (c i t) -> p c t i", i=4, t=PACK),
+                in0=scaled[:, :, chunks[c]].rearrange("p t (c i) -> p c t i", i=4),
+                in1=inv_sq[:, :, chunks[c]].rearrange("p t (c i) -> p c t i", i=4),
+                op=ALU.mult)
+
+        def last_product(c):
+            codes, scales = quantise(hid[c][:], CHUNK, "hid%d" % c)
+            acc = psum.tile([P, N // P, CHUNK], F32, name="basin%d" % c, tag="tm%d" % c)
+            for g in range(N // P):
+                cols = slice(g * P, (g + 1) * P)
+                nc.tensor.matmul_mx(
+                    out=acc[:, g, :], lhsT=w3_codes[:, cols].bitcast(FP8X4), lhsT_scale=w3_scales[:, cols],
+                    rhs=codes[:].bitcast(FP8X4), rhs_scale=scales[:], start=True, stop=True)
+            res = keep.tile([P, N // P, CHUNK], F32, name="res%d" % c)
+            nc.scalar.copy(out=res[:], in_=acc[:])
+            nc.sync.dma_start(out_view[:, :, chunks[c]], res[:])
+
+        round_hidden(0)
+        for c in range(len(chunks)):
+            if c + 1 < len(chunks):
+                round_hidden(c + 1)
+            last_product(c)

@@ -1,3 +1,4 @@
+import math
 from contextlib import ExitStack
 
 import concourse.mybir as mybir
@@ -48,6 +49,10 @@ def tile_picked_ypenman_et_p_kernel(
                 scale_table[32 * q : 32 * q + 4, :].bitcast(I32),
                 x_scales[0, 4 * q : 4 * q + 4, :].bitcast(I32),
             )
+        one = keep.tile([P, 1], F32, name="one")
+        nc.vector.memset(one[:], 1.0)
+        log_share = keep.tile([P, 1], F32, name="log_share")
+        nc.vector.tensor_scalar(out=log_share[:], in0=one[:], scalar1=math.log(0.6), scalar2=None, op0=ALU.mult)
         word_table = keep.tile([P, T], I32, name="word_table", tag="words_then_weights")
         nc.sync.dma_start(word_table[:], x_words[0].rearrange("p n t -> p (n t)").bitcast(I32))
         unit_sb = keep.tile([P, PACK], F32, name="unit_sb")
@@ -71,106 +76,129 @@ def tile_picked_ypenman_et_p_kernel(
         w1_codes, w1_scales = quantise(w1_grouped[:], H, "w1")
 
         w2_raw = keep.tile([P, PACK, H], F32, name="w2_raw", tag="raw")
-        nc.sync.dma_start(w2_raw[:], w2.rearrange("(p j) c -> p j c", j=PACK))
+        w2_view = w2.rearrange("(p j) c -> p j c", j=PACK)
+        for u in range(2):
+            cols = slice(u * H // 2, (u + 1) * H // 2)
+            nc.sync.dma_start(w2_raw[:, :, cols], w2_view[:, :, cols])
         wind_sb = keep.tile([P, PACK, S], F32, name="wind_sb", tag="grouped_then_wind", align_bytes=64)
-        nc.sync.dma_start(wind_sb[:], wind.rearrange("(p t) s -> p t s", t=PACK))
+        wind_view = wind.rearrange("(p t) s -> p t s", t=PACK)
+        for u in range(2):
+            nc.sync.dma_start(wind_sb[:, 2 * u : 2 * u + 2, :], wind_view[:, 2 * u : 2 * u + 2, :])
         x_scale = keep.tile([P, S], U8, name="x_scale", align_bytes=64)
         nc.vector.tensor_copy(out=x_scale[:], in_=scale_table[:].indirect(offs_sb[:]))
+        half = S // 2
+        halves = [slice(u * half, (u + 1) * half) for u in range(2)]
+        list_halves = [slice(u * half // LIST_ROWS, (u + 1) * half // LIST_ROWS) for u in range(2)]
         x_code = keep.tile([P, S], U32, name="x_code", align_bytes=64)
-        nc.vector.tensor_copy(out=x_code[:], in_=word_table[:].bitcast(U32).indirect(offs_sb[:]))
+        for u in range(2):
+            nc.vector.tensor_copy(
+                out=x_code[:, halves[u]], in_=word_table[:].bitcast(U32).indirect(offs_sb[:, list_halves[u]]))
 
         w3_raw = keep.tile([P, PACK, N], F32, name="w3_raw", tag="words_then_weights")
         nc.sync.dma_start(w3_raw[:], w3.rearrange("(p j) c -> p j c", j=PACK))
 
-        def first_product(codes, scales, t, tag):
-            acc = psum.tile([P, S], F32, name=tag, tag=tag)
+        def first_product(acc, codes, scales, t, days):
             cols = slice(t * P, (t + 1) * P)
             nc.tensor.matmul_mx(
-                out=acc[:], lhsT=codes[:, cols].bitcast(FP8X4), lhsT_scale=scales[:, cols],
-                rhs=x_code[:].bitcast(FP8X4), rhs_scale=x_scale[:], start=True, stop=True,
+                out=acc, lhsT=codes[:, cols].bitcast(FP8X4), lhsT_scale=scales[:, cols],
+                rhs=x_code[:, days].bitcast(FP8X4), rhs_scale=x_scale[:, days], start=True, stop=True,
             )
-            return acc
 
-        tm = [first_product(w1_codes, w1_scales, t, "tm%d" % t) for t in range(PACK)]
+        lo, hi = slice(0, 2), slice(2, 4)
+        tm = {}
+        for u in range(2):
+            for i, pair in enumerate((lo, hi)):
+                bank = psum.tile([P, 2, half], F32, name="tm%d%d" % (u, i), tag="tm%d" % (2 * u + i))
+                for t in range(pair.start, pair.stop):
+                    tm[t, u] = bank[:, t - pair.start, :]
+                    first_product(tm[t, u], w1_codes, w1_scales, t, halves[u])
 
-        th, root, ed = rows("th"), rows("root"), rows("ed")
-        h, wh, r, deficit = rows("h"), rows("wh"), rows("r"), rows("deficit")
+        square, inv_es, ed = rows("square"), rows("inv_es"), rows("ed")
+        g, r, moist = rows("g"), rows("r"), rows("moist")
         aero, part, den_unit = rows("aero"), rows("part"), rows("den_unit")
-        es = [keep.tile([P, S], F32, name="es%d" % t) for t in range(PACK)]
+        th = [keep.tile([P, S], F32, name="th%d" % t) for t in range(PACK)]
 
         w2_grouped, dst, src = dealt_views(w2_raw, "w2", "w2_grouped")
-        nc.vector.tensor_copy(out=dst, in_=src)
+        for u in range(2):
+            nc.vector.tensor_copy(out=dst[:, u * P // 2 : (u + 1) * P // 2], in_=src[:, u * P // 2 : (u + 1) * P // 2])
         w2_codes, w2_scales = quantise(w2_grouped[:], H, "w2")
-        rd = [first_product(w2_codes, w2_scales, t, "rd%d" % t) for t in range(PACK)]
+        rd = [psum.tile([P, S], F32, name="rd%d" % t) for t in range(PACK)]
+        for t in range(PACK):
+            first_product(rd[t][:], w2_codes, w2_scales, t, slice(0, S))
 
-        half = S // 2
-        lo, hi = slice(0, 2), slice(2, 4)
+        def temperature(t, u):
+            nc.scalar.activation(out=th[t][:, halves[u]], in_=tm[t, u], func=ACT.Tanh)
 
-        def saturation(t):
-            nc.scalar.activation(out=es[t][:], in_=th[:, t, :], func=ACT.Exp, scale=0.8)
+        def slope(t):
+            nc.scalar.activation(out=square[:, t, :], in_=th[t][:], func=ACT.Square, scale=0.3 / 1.3, bias=1.0)
+            nc.scalar.activation(out=inv_es[:, t, :], in_=th[t][:], func=ACT.Exp, scale=-0.8)
 
         def other_day(t):
             for u in range(2):
                 nc.scalar.activation(
-                    out=ed[:, t, u * half : (u + 1) * half],
-                    in_=es[t][:].indirect(stn_sb[:, u * half // LIST_ROWS : (u + 1) * half // LIST_ROWS]),
-                    func=ACT.Copy)
+                    out=ed[:, t, halves[u]], in_=th[t][:].indirect(stn_sb[:, list_halves[u]]),
+                    func=ACT.Exp, scale=0.8, bias=log_share[:])
 
-        for t in (0, 1):
-            nc.scalar.activation(out=th[:, t, :], in_=tm[t][:], func=ACT.Tanh)
-        nc.scalar.activation(out=root[:, lo, :], in_=th[:, lo, :], func=ACT.Exp, scale=-0.4)
-        for t in (0, 1):
-            saturation(t)
-        for t in (2, 3):
-            nc.scalar.activation(out=th[:, t, :], in_=tm[t][:], func=ACT.Tanh)
-        for t in (0, 1):
-            other_day(t)
-        nc.scalar.activation(out=h[:, hi, :], in_=th[:, hi, :], func=ACT.Square, scale=0.3 / 1.3, bias=1.0)
-        nc.scalar.activation(out=root[:, hi, :], in_=th[:, hi, :], func=ACT.Exp, scale=-0.8)
-        for t in (2, 3):
-            saturation(t)
-        for t in (2, 3):
-            other_day(t)
-
-        def ratio(pair, last, factor):
-            nc.vector.scalar_tensor_tensor(
-                out=wh[:, pair, :], in0=wind_sb[:, pair, :], scalar=0.5 / 0.3, in1=h[:, pair, :], op0=ALU.add, op1=ALU.mult)
+        for pair in (lo, hi):
+            for u in range(2):
+                for t in range(pair.start, pair.stop):
+                    temperature(t, u)
             for t in range(pair.start, pair.stop):
-                nc.vector.scalar_tensor_tensor(
-                    out=deficit[:, t, :], in0=ed[:, t, :], scalar=-0.6, in1=es[t][:], op0=ALU.mult, op1=ALU.add)
-            nc.vector.scalar_tensor_tensor(
-                out=r[:, pair, :], in0=wh[:, pair, :], scalar=factor, in1=last[:, pair, :], op0=ALU.mult, op1=ALU.mult)
-            nc.vector.scalar_tensor_tensor(
-                out=aero[:, pair, :], in0=deficit[:, pair, :], scalar=0.0, in1=wind_sb[:, pair, :], op0=ALU.max, op1=ALU.mult)
+                slope(t)
             for t in range(pair.start, pair.stop):
-                nc.vector.tensor_scalar(
-                    out=den_unit[:, t, :], in0=r[:, t, :], scalar1=-1.0, scalar2=unit_twice[:, t : t + 1],
-                    op0=ALU.is_ge, op1=ALU.mult)
-            nc.vector.tensor_tensor(out=wh[:, pair, :], in0=aero[:, pair, :], in1=r[:, pair, :], op=ALU.mult)
-
-        def partial(pair):
-            for t in range(pair.start, pair.stop):
-                nc.vector.scalar_tensor_tensor(
-                    out=part[:, t, :], in0=rd[t][:], scalar=0.0, in1=wh[:, t, :], op0=ALU.max, op1=ALU.add)
-
-        unit_twice = keep.tile([P, PACK], F32, name="unit_twice")
-        nc.vector.tensor_scalar(out=unit_twice[:], in0=unit_sb[:], scalar1=2.0, scalar2=None, op0=ALU.mult)
-        nc.vector.scalar_tensor_tensor(
-            out=h[:, lo, :], in0=th[:, lo, :], scalar=1.3 / 0.3, in1=root[:, lo, :], op0=ALU.add, op1=ALU.mult)
-        w3_grouped = keep.tile([P, PACK * N], BF16, name="w3_grouped", align_bytes=64)
-        nc.vector.tensor_copy(
-            out=w3_grouped[:].rearrange("p (c i j) -> p c j i", i=4, j=PACK),
-            in_=w3_raw[:].rearrange("p j (c i) -> p c j i", i=4))
-        ratio(lo, h, 0.3 ** 3)
-        w3_codes, w3_scales = quantise(w3_grouped[:], N, "w3")
-        partial(lo)
-        ratio(hi, root, 0.3 * 1.3 ** 2)
-        partial(hi)
+                other_day(t)
 
         rd_abs, decay = rows("rd_abs"), rows("decay")
         for t in range(PACK):
             nc.scalar.activation(out=rd_abs[:, t, :], in_=rd[t][:], func=ACT.Abs)
         nc.scalar.activation(out=decay[:], in_=rd_abs[:], func=ACT.Exp, scale=-1.0)
+
+        def ratio(tiles):
+            nc.vector.scalar_tensor_tensor(
+                out=g[:, tiles, :], in0=wind_sb[:, tiles, :], scalar=0.5 / 0.3, in1=square[:, tiles, :], op0=ALU.add, op1=ALU.mult)
+            nc.vector.scalar_tensor_tensor(
+                out=r[:, tiles, :], in0=g[:, tiles, :], scalar=0.3 * 1.3 ** 2, in1=inv_es[:, tiles, :], op0=ALU.mult, op1=ALU.mult)
+            nc.vector.scalar_tensor_tensor(
+                out=aero[:, tiles, :], in0=g[:, tiles, :], scalar=-0.3 * 1.3 ** 2, in1=wind_sb[:, tiles, :], op0=ALU.mult, op1=ALU.mult)
+            for t in range(tiles.start, tiles.stop):
+                nc.vector.tensor_scalar(
+                    out=den_unit[:, t, :], in0=r[:, t, :], scalar1=-1.0, scalar2=unit_twice[:, t : t + 1],
+                    op0=ALU.is_ge, op1=ALU.mult)
+
+        def moisture(pair):
+            nc.vector.tensor_tensor(out=moist[:, pair, :], in0=ed[:, pair, :], in1=inv_es[:, pair, :], op=ALU.mult)
+
+        def deficit(pair):
+            nc.vector.tensor_scalar(
+                out=ed[:, pair, :], in0=moist[:, pair, :], scalar1=1.0, scalar2=1.0, op0=ALU.min, op1=ALU.subtract)
+
+        def drying(pair):
+            nc.vector.tensor_tensor(out=moist[:, pair, :], in0=aero[:, pair, :], in1=ed[:, pair, :], op=ALU.mult)
+
+        def partial(pair):
+            for t in range(pair.start, pair.stop):
+                nc.vector.scalar_tensor_tensor(
+                    out=part[:, t, :], in0=rd[t][:], scalar=0.0, in1=moist[:, t, :], op0=ALU.max, op1=ALU.add)
+
+        unit_twice = keep.tile([P, PACK], F32, name="unit_twice")
+        nc.vector.tensor_scalar(out=unit_twice[:], in0=unit_sb[:], scalar1=2.0, scalar2=None, op0=ALU.mult)
+        w3_grouped = keep.tile([P, PACK * N], BF16, name="w3_grouped", align_bytes=64)
+        ratio(slice(0, 1))
+        ratio(slice(1, 2))
+        moisture(lo)
+        nc.vector.tensor_copy(
+            out=w3_grouped[:].rearrange("p (c i j) -> p c j i", i=4, j=PACK),
+            in_=w3_raw[:].rearrange("p j (c i) -> p c j i", i=4))
+        deficit(lo)
+        w3_codes, w3_scales = quantise(w3_grouped[:], N, "w3")
+        drying(lo)
+        ratio(hi)
+        moisture(hi)
+        partial(slice(0, 1))
+        deficit(hi)
+        partial(slice(1, 2))
+        drying(hi)
+        partial(hi)
 
         soft = rows("soft")
         for pair in (lo, hi):
@@ -179,7 +207,7 @@ def tile_picked_ypenman_et_p_kernel(
         num = aero
         for pair in (lo, hi):
             nc.vector.tensor_tensor(out=num[:, pair, :], in0=soft[:, pair, :], in1=part[:, pair, :], op=ALU.add)
-        scaled = deficit
+        scaled = moist
         for t in range(PACK):
             nc.vector.scalar_tensor_tensor(
                 out=scaled[:, t, :], in0=den_unit[:, t, :], scalar=unit_sb[:, t : t + 1], in1=num[:, t, :],
@@ -187,10 +215,12 @@ def tile_picked_ypenman_et_p_kernel(
 
         inv_sq = rows("inv_sq")
         chunks = [slice(c * CHUNK, (c + 1) * CHUNK) for c in range(S // CHUNK)]
-        for cols in chunks:
-            nc.scalar.activation(out=decay[:, :, cols], in_=r[:, :, cols], func=ACT.Abs_reciprocal_sqrt, bias=1.0)
-        for cols in chunks:
-            nc.scalar.activation(out=inv_sq[:, :, cols], in_=decay[:, :, cols], func=ACT.Square)
+        for c in range(len(chunks) + 1):
+            if c < len(chunks):
+                nc.scalar.activation(
+                    out=decay[:, :, chunks[c]], in_=r[:, :, chunks[c]], func=ACT.Abs_reciprocal_sqrt, bias=1.0)
+            if c > 0:
+                nc.scalar.activation(out=inv_sq[:, :, chunks[c - 1]], in_=decay[:, :, chunks[c - 1]], func=ACT.Square)
         hid = [keep.tile([P, PACK * CHUNK], BF16, name="hid%d" % c, align_bytes=64) for c in range(len(chunks))]
         out_view = out.rearrange("(g m) j -> m g j", m=P)
 
@@ -204,10 +234,10 @@ def tile_picked_ypenman_et_p_kernel(
         def last_product(c):
             codes, scales = quantise(hid[c][:], CHUNK, "hid%d" % c)
             acc = psum.tile([P, N // P, CHUNK], F32, name="basin%d" % c, tag="tm%d" % c)
-            for g in range(N // P):
-                cols = slice(g * P, (g + 1) * P)
+            for b in range(N // P):
+                cols = slice(b * P, (b + 1) * P)
                 nc.tensor.matmul_mx(
-                    out=acc[:, g, :], lhsT=w3_codes[:, cols].bitcast(FP8X4), lhsT_scale=w3_scales[:, cols],
+                    out=acc[:, b, :], lhsT=w3_codes[:, cols].bitcast(FP8X4), lhsT_scale=w3_scales[:, cols],
                     rhs=codes[:].bitcast(FP8X4), rhs_scale=scales[:], start=True, stop=True)
             res = keep.tile([P, N // P, CHUNK], F32, name="res%d" % c)
             nc.scalar.copy(out=res[:], in_=acc[:])

@@ -19,8 +19,8 @@ ALU = mybir.AluOpType
 P = 128
 PACK = 4
 LIST_ROWS = 16
-CHUNK = 128
-SCALAR_CAST = 64
+EDGES = (0, 128, 256, 384, 448, 512)
+SCALAR_CAST = 32
 
 
 def tile_picked_ypenman_et_p_kernel(
@@ -66,12 +66,12 @@ def tile_picked_ypenman_et_p_kernel(
 
         def dealt_views(raw, name, tag):
             grouped = keep.tile([P, PACK * H], BF16, name=name + "_grouped", tag=tag, align_bytes=64)
-            dst = grouped[:].rearrange("p (t m j) -> p m j t", t=PACK, j=PACK)
-            src = raw[:].rearrange("p j (m t) -> p m j t", t=PACK)
+            dst = grouped[:].rearrange("p (t n e j) -> p n j e t", t=PACK, e=2, j=PACK)
+            src = raw[:].rearrange("p j (n e t) -> p n j e t", e=2, t=PACK)
             return grouped, dst, src
 
         w1_grouped, dst, src = dealt_views(w1_raw, "w1", "grouped_then_wind")
-        nc.scalar.activation(out=dst[:, :SCALAR_CAST], in_=src[:, :SCALAR_CAST], func=ACT.Copy)
+        nc.scalar.copy(out=dst[:, :SCALAR_CAST], in_=src[:, :SCALAR_CAST])
         nc.vector.tensor_copy(out=dst[:, SCALAR_CAST:], in_=src[:, SCALAR_CAST:])
         w1_codes, w1_scales = quantise(w1_grouped[:], H, "w1")
 
@@ -113,14 +113,16 @@ def tile_picked_ypenman_et_p_kernel(
                     tm[t, u] = bank[:, t - pair.start, :]
                     first_product(tm[t, u], w1_codes, w1_scales, t, halves[u])
 
-        square, inv_es, ed = rows("square"), rows("inv_es"), rows("ed")
+        square, inv_es = rows("square"), rows("inv_es")
+        ed = keep.tile([P, PACK, S], F32, name="ed", tag="ed", align_bytes=64)
         g, r, moist = rows("g"), rows("r"), rows("moist")
-        aero, part, den_unit = rows("aero"), rows("part"), rows("den_unit")
+        aero, den_unit = rows("aero"), rows("den_unit")
+        part = [moist[:, (t + 2) % PACK, :] for t in range(PACK)]
         th = [keep.tile([P, S], F32, name="th%d" % t) for t in range(PACK)]
 
         w2_grouped, dst, src = dealt_views(w2_raw, "w2", "w2_grouped")
         for u in range(2):
-            nc.vector.tensor_copy(out=dst[:, u * P // 2 : (u + 1) * P // 2], in_=src[:, u * P // 2 : (u + 1) * P // 2])
+            nc.vector.tensor_copy(out=dst[:, u * P // 4 : (u + 1) * P // 4], in_=src[:, u * P // 4 : (u + 1) * P // 4])
         w2_codes, w2_scales = quantise(w2_grouped[:], H, "w2")
         rd = [psum.tile([P, S], F32, name="rd%d" % t) for t in range(PACK)]
         for t in range(PACK):
@@ -139,6 +141,7 @@ def tile_picked_ypenman_et_p_kernel(
                     out=ed[:, t, halves[u]], in_=th[t][:].indirect(stn_sb[:, list_halves[u]]),
                     func=ACT.Exp, scale=0.8, bias=log_share[:])
 
+        rd_abs, decay = rows("rd_abs"), rows("decay")
         for pair in (lo, hi):
             for u in range(2):
                 for t in range(pair.start, pair.stop):
@@ -147,8 +150,6 @@ def tile_picked_ypenman_et_p_kernel(
                 slope(t)
             for t in range(pair.start, pair.stop):
                 other_day(t)
-
-        rd_abs, decay = rows("rd_abs"), rows("decay")
         for t in range(PACK):
             nc.scalar.activation(out=rd_abs[:, t, :], in_=rd[t][:], func=ACT.Abs)
         nc.scalar.activation(out=decay[:], in_=rd_abs[:], func=ACT.Exp, scale=-1.0)
@@ -160,10 +161,11 @@ def tile_picked_ypenman_et_p_kernel(
                 out=r[:, tiles, :], in0=g[:, tiles, :], scalar=0.3 * 1.3 ** 2, in1=inv_es[:, tiles, :], op0=ALU.mult, op1=ALU.mult)
             nc.vector.scalar_tensor_tensor(
                 out=aero[:, tiles, :], in0=g[:, tiles, :], scalar=-0.3 * 1.3 ** 2, in1=wind_sb[:, tiles, :], op0=ALU.mult, op1=ALU.mult)
-            for t in range(tiles.start, tiles.stop):
-                nc.vector.tensor_scalar(
-                    out=den_unit[:, t, :], in0=r[:, t, :], scalar1=-1.0, scalar2=unit_twice[:, t : t + 1],
-                    op0=ALU.is_ge, op1=ALU.mult)
+
+        def sign(t):
+            nc.vector.tensor_scalar(
+                out=den_unit[:, t, :], in0=r[:, t, :], scalar1=-1.0, scalar2=unit_twice[:, t : t + 1],
+                op0=ALU.is_ge, op1=ALU.mult)
 
         def moisture(pair):
             nc.vector.tensor_tensor(out=moist[:, pair, :], in0=ed[:, pair, :], in1=inv_es[:, pair, :], op=ALU.mult)
@@ -172,56 +174,64 @@ def tile_picked_ypenman_et_p_kernel(
             nc.vector.tensor_scalar(
                 out=ed[:, pair, :], in0=moist[:, pair, :], scalar1=1.0, scalar2=1.0, op0=ALU.min, op1=ALU.subtract)
 
-        def drying(pair):
-            nc.vector.tensor_tensor(out=moist[:, pair, :], in0=aero[:, pair, :], in1=ed[:, pair, :], op=ALU.mult)
+        def drying(engine, pair):
+            engine.tensor_tensor(out=g[:, pair, :], in0=aero[:, pair, :], in1=ed[:, pair, :], op=ALU.mult)
 
         def partial(pair):
             for t in range(pair.start, pair.stop):
                 nc.vector.scalar_tensor_tensor(
-                    out=part[:, t, :], in0=rd[t][:], scalar=0.0, in1=moist[:, t, :], op0=ALU.max, op1=ALU.add)
+                    out=part[t], in0=rd[t][:], scalar=0.0, in1=g[:, t, :], op0=ALU.max, op1=ALU.add)
 
         unit_twice = keep.tile([P, PACK], F32, name="unit_twice")
         nc.vector.tensor_scalar(out=unit_twice[:], in0=unit_sb[:], scalar1=2.0, scalar2=None, op0=ALU.mult)
-        w3_grouped = keep.tile([P, PACK * N], BF16, name="w3_grouped", align_bytes=64)
         ratio(slice(0, 1))
         ratio(slice(1, 2))
+        sign(0)
         moisture(lo)
-        nc.vector.tensor_copy(
-            out=w3_grouped[:].rearrange("p (c i j) -> p c j i", i=4, j=PACK),
-            in_=w3_raw[:].rearrange("p j (c i) -> p c j i", i=4))
+        sign(1)
         deficit(lo)
-        w3_codes, w3_scales = quantise(w3_grouped[:], N, "w3")
-        drying(lo)
         ratio(hi)
+        drying(nc.vector, lo)
         moisture(hi)
-        partial(slice(0, 1))
+        sign(2)
+        sign(3)
         deficit(hi)
-        partial(slice(1, 2))
-        drying(hi)
+        drying(nc.gpsimd, slice(3, 4))
+        partial(lo)
+        drying(nc.vector, slice(2, 3))
+        w3_grouped = keep.tile([P, PACK * N], BF16, name="w3_grouped", tag="ed", align_bytes=64)
+        nc.gpsimd.tensor_scalar(
+            out=w3_grouped[:].rearrange("p (c i j) -> p c j i", i=4, j=PACK),
+            in0=w3_raw[:].rearrange("p j (c i) -> p c j i", i=4),
+            scalar1=1.0, scalar2=0.0, op0=ALU.mult, op1=ALU.add)
         partial(hi)
 
         soft = rows("soft")
-        for pair in (lo, hi):
+        groups = (slice(0, 1), slice(1, 2), hi)
+        for pair in groups:
             nc.scalar.activation(out=soft[:, pair, :], in_=decay[:, pair, :], func=ACT.Ln, bias=1.0)
 
         num = aero
-        for pair in (lo, hi):
-            nc.vector.tensor_tensor(out=num[:, pair, :], in0=soft[:, pair, :], in1=part[:, pair, :], op=ALU.add)
-        scaled = moist
+        for pair in groups:
+            swapped = slice((pair.start + 2) % PACK, (pair.stop + 1) % PACK + 1)
+            nc.vector.tensor_tensor(out=num[:, pair, :], in0=soft[:, pair, :], in1=moist[:, swapped, :], op=ALU.add)
+        w3_codes, w3_scales = quantise(w3_grouped[:], N, "w3")
+        scaled = square
         for t in range(PACK):
             nc.vector.scalar_tensor_tensor(
                 out=scaled[:, t, :], in0=den_unit[:, t, :], scalar=unit_sb[:, t : t + 1], in1=num[:, t, :],
                 op0=ALU.subtract, op1=ALU.mult)
 
         inv_sq = rows("inv_sq")
-        chunks = [slice(c * CHUNK, (c + 1) * CHUNK) for c in range(S // CHUNK)]
+        chunks = [slice(a, b) for a, b in zip(EDGES, EDGES[1:])]
+        widths = [b - a for a, b in zip(EDGES, EDGES[1:])]
         for c in range(len(chunks) + 1):
             if c < len(chunks):
                 nc.scalar.activation(
                     out=decay[:, :, chunks[c]], in_=r[:, :, chunks[c]], func=ACT.Abs_reciprocal_sqrt, bias=1.0)
             if c > 0:
                 nc.scalar.activation(out=inv_sq[:, :, chunks[c - 1]], in_=decay[:, :, chunks[c - 1]], func=ACT.Square)
-        hid = [keep.tile([P, PACK * CHUNK], BF16, name="hid%d" % c, align_bytes=64) for c in range(len(chunks))]
+        hid = [keep.tile([P, PACK * widths[c]], BF16, name="hid%d" % c, align_bytes=64) for c in range(len(chunks))]
         out_view = out.rearrange("(g m) j -> m g j", m=P)
 
         def round_hidden(c):
@@ -232,14 +242,14 @@ def tile_picked_ypenman_et_p_kernel(
                 op=ALU.mult)
 
         def last_product(c):
-            codes, scales = quantise(hid[c][:], CHUNK, "hid%d" % c)
-            acc = psum.tile([P, N // P, CHUNK], F32, name="basin%d" % c, tag="tm%d" % c)
+            codes, scales = quantise(hid[c][:], widths[c], "hid%d" % c)
+            acc = psum.tile([P, N // P, widths[c]], F32, name="basin%d" % c, tag="tm%d" % (c % 4))
             for b in range(N // P):
                 cols = slice(b * P, (b + 1) * P)
                 nc.tensor.matmul_mx(
                     out=acc[:, b, :], lhsT=w3_codes[:, cols].bitcast(FP8X4), lhsT_scale=w3_scales[:, cols],
                     rhs=codes[:].bitcast(FP8X4), rhs_scale=scales[:], start=True, stop=True)
-            res = keep.tile([P, N // P, CHUNK], F32, name="res%d" % c)
+            res = keep.tile([P, N // P, widths[c]], F32, name="res%d" % c)
             nc.scalar.copy(out=res[:], in_=acc[:])
             nc.sync.dma_start(out_view[:, :, chunks[c]], res[:])
 

import math
from contextlib import ExitStack

import concourse.mybir as mybir

K, T, S, N, H = 512, 2048, 512, 256, 512
FLOPS = 2 * K * H * S * 2 + 2 * H * N * S

F32 = mybir.dt.float32
BF16 = mybir.dt.bfloat16
I32 = mybir.dt.int32
U32 = mybir.dt.uint32
U16 = mybir.dt.uint16
U8 = mybir.dt.uint8
FP8X4 = mybir.dt.float8_e4m3fn_x4
ACT = mybir.ActivationFunctionType
ALU = mybir.AluOpType

P = 128
PACK = 4
LIST_ROWS = 16
EDGES = (0, 128, 256, 384, 448, 512)
SCALAR_CAST = 32


def tile_picked_ypenman_et_p_kernel(
    tc, x_words, x_scales, w1, w2, wind, unit, w3, offs, stn, out
):
    nc = tc.nc
    with ExitStack() as ctx:
        keep = ctx.enter_context(tc.tile_pool(name="keep", bufs=1))
        psum = ctx.enter_context(tc.psum_pool(name="psum", bufs=1))

        def rows(name):
            return keep.tile([P, PACK, S], F32, name=name)

        offs_sb = keep.tile([P, S // LIST_ROWS], U16, name="offs_sb")
        nc.sync.dma_start(offs_sb[:], offs)
        stn_sb = keep.tile([P, S // LIST_ROWS], U16, name="stn_sb")
        nc.sync.dma_start(stn_sb[:], stn)

        w1_raw = keep.tile([P, PACK, H], F32, name="w1_raw", tag="raw")
        nc.sync.dma_start(w1_raw[:], w1.rearrange("(p j) c -> p j c", j=PACK))

        scale_table = keep.tile([P, T], U8, name="scale_table")
        nc.gpsimd.memset(scale_table[:].bitcast(I32), 0)
        for q in range(4):
            nc.sync.dma_start(
                scale_table[32 * q : 32 * q + 4, :].bitcast(I32),
                x_scales[0, 4 * q : 4 * q + 4, :].bitcast(I32),
            )
        one = keep.tile([P, 1], F32, name="one")
        nc.vector.memset(one[:], 1.0)
        log_share = keep.tile([P, 1], F32, name="log_share")
        nc.vector.tensor_scalar(out=log_share[:], in0=one[:], scalar1=math.log(0.6), scalar2=None, op0=ALU.mult)
        word_table = keep.tile([P, T], I32, name="word_table", tag="words_then_weights")
        nc.sync.dma_start(word_table[:], x_words[0].rearrange("p n t -> p (n t)").bitcast(I32))
        unit_sb = keep.tile([P, PACK], F32, name="unit_sb")
        nc.sync.dma_start(unit_sb[:], unit.rearrange("(p t) o -> p (t o)", t=PACK))

        def quantise(grouped, width, name):
            codes = keep.tile([P, width], U32, name=name + "_codes", align_bytes=64)
            scales = keep.tile([P, width], U8, name=name + "_scales", align_bytes=64)
            nc.vector.quantize_mx(out=codes[:].bitcast(FP8X4), scales=scales[:], in_=grouped)
            return codes, scales

        def dealt_views(raw, name, tag):
            grouped = keep.tile([P, PACK * H], BF16, name=name + "_grouped", tag=tag, align_bytes=64)
            dst = grouped[:].rearrange("p (t n e j) -> p n j e t", t=PACK, e=2, j=PACK)
            src = raw[:].rearrange("p j (n e t) -> p n j e t", e=2, t=PACK)
            return grouped, dst, src

        w1_grouped, dst, src = dealt_views(w1_raw, "w1", "grouped_then_wind")
        nc.scalar.copy(out=dst[:, :SCALAR_CAST], in_=src[:, :SCALAR_CAST])
        nc.vector.tensor_copy(out=dst[:, SCALAR_CAST:], in_=src[:, SCALAR_CAST:])
        w1_codes, w1_scales = quantise(w1_grouped[:], H, "w1")

        w2_raw = keep.tile([P, PACK, H], F32, name="w2_raw", tag="raw")
        w2_view = w2.rearrange("(p j) c -> p j c", j=PACK)
        for u in range(2):
            cols = slice(u * H // 2, (u + 1) * H // 2)
            nc.sync.dma_start(w2_raw[:, :, cols], w2_view[:, :, cols])
        wind_sb = keep.tile([P, PACK, S], F32, name="wind_sb", tag="grouped_then_wind", align_bytes=64)
        wind_view = wind.rearrange("(p t) s -> p t s", t=PACK)
        for u in range(2):
            nc.sync.dma_start(wind_sb[:, 2 * u : 2 * u + 2, :], wind_view[:, 2 * u : 2 * u + 2, :])
        x_scale = keep.tile([P, S], U8, name="x_scale", align_bytes=64)
        nc.vector.tensor_copy(out=x_scale[:], in_=scale_table[:].indirect(offs_sb[:]))
        half = S // 2
        halves = [slice(u * half, (u + 1) * half) for u in range(2)]
        list_halves = [slice(u * half // LIST_ROWS, (u + 1) * half // LIST_ROWS) for u in range(2)]
        x_code = keep.tile([P, S], U32, name="x_code", align_bytes=64)
        for u in range(2):
            nc.vector.tensor_copy(
                out=x_code[:, halves[u]], in_=word_table[:].bitcast(U32).indirect(offs_sb[:, list_halves[u]]))

        w3_raw = keep.tile([P, PACK, N], F32, name="w3_raw", tag="words_then_weights")
        nc.sync.dma_start(w3_raw[:], w3.rearrange("(p j) c -> p j c", j=PACK))

        def first_product(acc, codes, scales, t, days):
            cols = slice(t * P, (t + 1) * P)
            nc.tensor.matmul_mx(
                out=acc, lhsT=codes[:, cols].bitcast(FP8X4), lhsT_scale=scales[:, cols],
                rhs=x_code[:, days].bitcast(FP8X4), rhs_scale=x_scale[:, days], start=True, stop=True,
            )

        lo, hi = slice(0, 2), slice(2, 4)
        tm = {}
        for u in range(2):
            for i, pair in enumerate((lo, hi)):
                bank = psum.tile([P, 2, half], F32, name="tm%d%d" % (u, i), tag="tm%d" % (2 * u + i))
                for t in range(pair.start, pair.stop):
                    tm[t, u] = bank[:, t - pair.start, :]
                    first_product(tm[t, u], w1_codes, w1_scales, t, halves[u])

        square, inv_es = rows("square"), rows("inv_es")
        ed = keep.tile([P, PACK, S], F32, name="ed", tag="ed", align_bytes=64)
        g, r, moist = rows("g"), rows("r"), rows("moist")
        aero, den_unit = rows("aero"), rows("den_unit")
        part = [moist[:, (t + 2) % PACK, :] for t in range(PACK)]
        th = [keep.tile([P, S], F32, name="th%d" % t) for t in range(PACK)]

        w2_grouped, dst, src = dealt_views(w2_raw, "w2", "w2_grouped")
        for u in range(2):
            nc.vector.tensor_copy(out=dst[:, u * P // 4 : (u + 1) * P // 4], in_=src[:, u * P // 4 : (u + 1) * P // 4])
        w2_codes, w2_scales = quantise(w2_grouped[:], H, "w2")
        rd = [psum.tile([P, S], F32, name="rd%d" % t) for t in range(PACK)]
        for t in range(PACK):
            first_product(rd[t][:], w2_codes, w2_scales, t, slice(0, S))

        def temperature(t, u):
            nc.scalar.activation(out=th[t][:, halves[u]], in_=tm[t, u], func=ACT.Tanh)

        def slope(t):
            nc.scalar.activation(out=square[:, t, :], in_=th[t][:], func=ACT.Square, scale=0.3 / 1.3, bias=1.0)
            nc.scalar.activation(out=inv_es[:, t, :], in_=th[t][:], func=ACT.Exp, scale=-0.8)

        def other_day(t):
            for u in range(2):
                nc.scalar.activation(
                    out=ed[:, t, halves[u]], in_=th[t][:].indirect(stn_sb[:, list_halves[u]]),
                    func=ACT.Exp, scale=0.8, bias=log_share[:])

        rd_abs, decay = rows("rd_abs"), rows("decay")
        for pair in (lo, hi):
            for u in range(2):
                for t in range(pair.start, pair.stop):
                    temperature(t, u)
            for t in range(pair.start, pair.stop):
                slope(t)
            for t in range(pair.start, pair.stop):
                other_day(t)
        for t in range(PACK):
            nc.scalar.activation(out=rd_abs[:, t, :], in_=rd[t][:], func=ACT.Abs)
        nc.scalar.activation(out=decay[:], in_=rd_abs[:], func=ACT.Exp, scale=-1.0)

        def ratio(tiles):
            nc.vector.scalar_tensor_tensor(
                out=g[:, tiles, :], in0=wind_sb[:, tiles, :], scalar=0.5 / 0.3, in1=square[:, tiles, :], op0=ALU.add, op1=ALU.mult)
            nc.vector.scalar_tensor_tensor(
                out=r[:, tiles, :], in0=g[:, tiles, :], scalar=0.3 * 1.3 ** 2, in1=inv_es[:, tiles, :], op0=ALU.mult, op1=ALU.mult)
            nc.vector.scalar_tensor_tensor(
                out=aero[:, tiles, :], in0=g[:, tiles, :], scalar=-0.3 * 1.3 ** 2, in1=wind_sb[:, tiles, :], op0=ALU.mult, op1=ALU.mult)

        def sign(t):
            nc.vector.tensor_scalar(
                out=den_unit[:, t, :], in0=r[:, t, :], scalar1=-1.0, scalar2=unit_twice[:, t : t + 1],
                op0=ALU.is_ge, op1=ALU.mult)

        def moisture(pair):
            nc.vector.tensor_tensor(out=moist[:, pair, :], in0=ed[:, pair, :], in1=inv_es[:, pair, :], op=ALU.mult)

        def deficit(pair):
            nc.vector.tensor_scalar(
                out=ed[:, pair, :], in0=moist[:, pair, :], scalar1=1.0, scalar2=1.0, op0=ALU.min, op1=ALU.subtract)

        def drying(engine, pair):
            engine.tensor_tensor(out=g[:, pair, :], in0=aero[:, pair, :], in1=ed[:, pair, :], op=ALU.mult)

        def partial(pair):
            for t in range(pair.start, pair.stop):
                nc.vector.scalar_tensor_tensor(
                    out=part[t], in0=rd[t][:], scalar=0.0, in1=g[:, t, :], op0=ALU.max, op1=ALU.add)

        unit_twice = keep.tile([P, PACK], F32, name="unit_twice")
        nc.vector.tensor_scalar(out=unit_twice[:], in0=unit_sb[:], scalar1=2.0, scalar2=None, op0=ALU.mult)
        ratio(slice(0, 1))
        ratio(slice(1, 2))
        sign(0)
        moisture(lo)
        sign(1)
        deficit(lo)
        ratio(hi)
        drying(nc.vector, lo)
        moisture(hi)
        sign(2)
        sign(3)
        deficit(hi)
        drying(nc.gpsimd, slice(3, 4))
        partial(lo)
        drying(nc.vector, slice(2, 3))
        w3_grouped = keep.tile([P, PACK * N], BF16, name="w3_grouped", tag="ed", align_bytes=64)
        nc.gpsimd.tensor_scalar(
            out=w3_grouped[:].rearrange("p (c i j) -> p c j i", i=4, j=PACK),
            in0=w3_raw[:].rearrange("p j (c i) -> p c j i", i=4),
            scalar1=1.0, scalar2=0.0, op0=ALU.mult, op1=ALU.add)
        partial(hi)

        soft = rows("soft")
        groups = (slice(0, 1), slice(1, 2), hi)
        for pair in groups:
            nc.scalar.activation(out=soft[:, pair, :], in_=decay[:, pair, :], func=ACT.Ln, bias=1.0)

        num = aero
        for pair in groups:
            swapped = slice((pair.start + 2) % PACK, (pair.stop + 1) % PACK + 1)
            nc.vector.tensor_tensor(out=num[:, pair, :], in0=soft[:, pair, :], in1=moist[:, swapped, :], op=ALU.add)
        w3_codes, w3_scales = quantise(w3_grouped[:], N, "w3")
        scaled = square
        for t in range(PACK):
            nc.vector.scalar_tensor_tensor(
                out=scaled[:, t, :], in0=den_unit[:, t, :], scalar=unit_sb[:, t : t + 1], in1=num[:, t, :],
                op0=ALU.subtract, op1=ALU.mult)

        inv_sq = rows("inv_sq")
        chunks = [slice(a, b) for a, b in zip(EDGES, EDGES[1:])]
        widths = [b - a for a, b in zip(EDGES, EDGES[1:])]
        for c in range(len(chunks) + 1):
            if c < len(chunks):
                nc.scalar.activation(
                    out=decay[:, :, chunks[c]], in_=r[:, :, chunks[c]], func=ACT.Abs_reciprocal_sqrt, bias=1.0)
            if c > 0:
                nc.scalar.activation(out=inv_sq[:, :, chunks[c - 1]], in_=decay[:, :, chunks[c - 1]], func=ACT.Square)
        hid = [keep.tile([P, PACK * widths[c]], BF16, name="hid%d" % c, align_bytes=64) for c in range(len(chunks))]
        out_view = out.rearrange("(g m) j -> m g j", m=P)

        def round_hidden(c):
            nc.vector.tensor_tensor(
                out=hid[c][:].rearrange("p (c i t) -> p c t i", i=4, t=PACK),
                in0=scaled[:, :, chunks[c]].rearrange("p t (c i) -> p c t i", i=4),
                in1=inv_sq[:, :, chunks[c]].rearrange("p t (c i) -> p c t i", i=4),
                op=ALU.mult)

        def last_product(c):
            codes, scales = quantise(hid[c][:], widths[c], "hid%d" % c)
            acc = psum.tile([P, N // P, widths[c]], F32, name="basin%d" % c, tag="tm%d" % (c % 4))
            for b in range(N // P):
                cols = slice(b * P, (b + 1) * P)
                nc.tensor.matmul_mx(
                    out=acc[:, b, :], lhsT=w3_codes[:, cols].bitcast(FP8X4), lhsT_scale=w3_scales[:, cols],
                    rhs=codes[:].bitcast(FP8X4), rhs_scale=scales[:], start=True, stop=True)
            res = keep.tile([P, N // P, widths[c]], F32, name="res%d" % c)
            nc.scalar.copy(out=res[:], in_=acc[:])
            nc.sync.dma_start(out_view[:, :, chunks[c]], res[:])

        round_hidden(0)
        for c in range(len(chunks)):
            if c + 1 < len(chunks):
                round_hidden(c + 1)
            last_product(c)
